import numpy as np
import ml_dtypes


def mxq(x, axis, fmt="e4m3"):
    dtype, down = {"e4m3": (ml_dtypes.float8_e4m3fn, 7), "e5m2": (ml_dtypes.float8_e5m2, 14)}[fmt]
    v = np.moveaxis(np.asarray(x, np.float32).astype(ml_dtypes.bfloat16).astype(np.float64), axis, -1)
    blocks = v.reshape(v.shape[:-1] + (-1, 32))
    amax = np.abs(blocks).max(-1, keepdims=True)
    byte = np.maximum(np.where(amax > 0, np.frexp(amax)[1] - 1 + 127, 0) - down, 1)
    scale = np.exp2(byte - 127.0)
    codes = (blocks / scale).astype(np.float32).astype(dtype).astype(np.float64)
    return np.moveaxis((codes * scale).reshape(v.shape), -1, axis)


WIDE = False


def mx_kscale(k):
    if not WIDE:
        return np.ones(k)
    levels = np.array([10, -10, 5, -5, 0])
    if k % 512:
        return np.exp2(np.random.permutation(np.resize(levels, k // 32))).repeat(32)
    a = np.empty((k // 512, 16))
    for p in range(k // 512):
        a[p, :8] = np.random.permutation(np.resize(levels, 8))
        for g in range(8):
            far = levels[np.abs(levels - a[p, g]) >= 10]
            a[p, g + 8] = far[np.random.randint(len(far))]
    return np.exp2(a.ravel()).repeat(32)


def f64(x):
    return np.asarray(x).astype(np.float64)


def striped(idx):
    return np.tile(idx.reshape(-1, 16).T, (8, 1)).astype(np.uint16)


def unstriped(offs):
    return offs[:16].T.reshape(-1).astype(np.int64)


E2M1 = np.array([0.0, 0.5, 1.0, 1.5, 2.0, 3.0, 4.0, 6.0, -0.0, -0.5, -1.0, -1.5, -2.0, -3.0, -4.0, -6.0])


def pack_weight(w, fmt):
    k, n = w.shape
    w = f64(np.asarray(w, np.float32).astype(ml_dtypes.bfloat16)).reshape(k // 32, 32, n)
    amax = np.abs(w).max(1)
    if fmt == "e4m3":
        byte = np.frexp(amax)[1] - 1 + 127 - 7
    else:
        mant, ex = np.frexp(amax / 6.0)
        byte = np.where(mant > 0.5, ex, ex - 1) + 127
    byte = np.clip(np.where(amax > 0, byte, 1), 1, 254)
    scaled = (w * np.exp2(127.0 - byte)[:, None, :]).reshape(k, n).astype(np.float32)
    by_word = np.ascontiguousarray(scaled.reshape(k // 512, 128, 4, n).transpose(0, 1, 3, 2))
    if fmt == "e4m3":
        words = by_word.astype(ml_dtypes.float8_e4m3fn).view(np.uint8)
    else:
        c = by_word.astype(ml_dtypes.float4_e2m1fn).view(np.uint8) & 0xF
        words = (c[..., 0::2] | (c[..., 1::2] << 4)).reshape(k // 512, 128, 2 * n)
    return np.ascontiguousarray(words), np.ascontiguousarray(byte.astype(np.uint8).reshape(k // 512, 16, n))


def unpack_weight(words, scales, fmt):
    g, _, n = scales.shape
    words = np.ascontiguousarray(words).reshape(g, 128, n, -1)
    if fmt == "e4m3":
        vals = words.view(ml_dtypes.float8_e4m3fn).astype(np.float64)
    else:
        nib = np.empty((g, 128, n, 4), np.uint8)
        nib[..., 0::2] = words & 0xF
        nib[..., 1::2] = words >> 4
        vals = E2M1[nib]
    vals = vals * np.repeat(np.exp2(scales.astype(np.float64) - 127.0), 8, axis=1)[..., None]
    return vals.transpose(0, 1, 3, 2).reshape(g * 512, n)


def sigmoid(v):
    return 1.0 / (1.0 + np.exp(-np.maximum(v, -700.0)))


K, T, E, C, H, N = 512, 1536, 6, 128, 512, 256


def by_expert(wq, xq):
    return np.concatenate([wq[e].T @ xq[:, e * C:(e + 1) * C] for e in range(E)], axis=1)


def setup_inputs():
    n = np.random.standard_normal
    s = mx_kscale(K)[:, None]
    u = mx_kscale(H)
    w1 = [pack_weight(m, "e2m1") for m in n((E, K, H)) / np.sqrt(K) / s[None]]
    w3 = [pack_weight(m, "e2m1") for m in n((E, K, H)) / np.sqrt(K) / s[None] * u[None, None, :]]
    w2 = [pack_weight(m, "e2m1") for m in n((E, H, N)) / np.sqrt(H) / u[None, :, None]]
    return {
        "xT": (n((K, T)) * s).astype(np.float32),
        "w1_words": np.stack([m[0] for m in w1]),
        "w1_scales": np.stack([m[1] for m in w1]),
        "w3_words": np.stack([m[0] for m in w3]),
        "w3_scales": np.stack([m[1] for m in w3]),
        "w2_words": np.stack([m[0] for m in w2]),
        "w2_scales": np.stack([m[1] for m in w2]),
        "gate": np.tile(np.random.uniform(0.2, 1.0, E * C), (N, 1)).astype(np.float32),
        "offs": striped(np.random.permutation(T)[:E * C]),
        "dst": striped(np.random.permutation(T)[:E * C]),
    }


def reference(xT, w1_words, w1_scales, w3_words, w3_scales, w2_words, w2_scales, gate, offs, dst):
    idx = unstriped(offs)
    w1 = np.stack([unpack_weight(w1_words[e], w1_scales[e], "e2m1") for e in range(E)])
    w3 = np.stack([unpack_weight(w3_words[e], w3_scales[e], "e2m1") for e in range(E)])
    w2 = np.stack([unpack_weight(w2_words[e], w2_scales[e], "e2m1") for e in range(E)])
    xq = mxq(f64(xT)[:, idx], 0, "e4m3")
    h = sigmoid(by_expert(w1, xq))
    h = h * by_expert(w3, xq)
    y = by_expert(w2, mxq(h, 0, "e4m3"))
    out = np.zeros((N, T))
    out[:, unstriped(dst)] = f64(gate) * y
    return out

@@ -1,0 +1,204 @@
+from contextlib import ExitStack
+
+import concourse.mybir as mybir
+from concourse.masks import make_identity
+
+K, T, E, C, H, N = 512, 1536, 6, 128, 512, 256
+FLOPS = 2 * E * C * (2 * K * H + H * N)
+
+F32 = mybir.dt.float32
+BF16 = mybir.dt.bfloat16
+I32 = mybir.dt.int32
+U32 = mybir.dt.uint32
+U16 = mybir.dt.uint16
+U8 = mybir.dt.uint8
+FP8X4 = mybir.dt.float8_e4m3fn_x4
+FP4X4 = mybir.dt.float4_e2m1fn_x4
+ACT = mybir.ActivationFunctionType
+MULT = mybir.AluOpType.mult
+
+P = 128
+G = 3
+GS = 2 * C
+GO = GS // 16
+
+
+def tile_moe_two_glu_sigmoid_kernel(
+    tc, xT, w1_words, w1_scales, w3_words, w3_scales, w2_words, w2_scales, gate, offs, dst, out
+):
+    nc = tc.nc
+    with ExitStack() as ctx:
+        keep = ctx.enter_context(tc.tile_pool(name="keep", bufs=1))
+        work = ctx.enter_context(tc.tile_pool(name="work", bufs=3))
+        psum = ctx.enter_context(tc.psum_pool(name="psum", bufs=2))
+
+        offs_sb = keep.tile([P, E * C // 16], U16, name="offs_sb")
+        dst_sb = keep.tile([P, E * C // 16], U16, name="dst_sb")
+        warm = keep.tile([P, 1], F32, name="warm")
+        ident = keep.tile([P, P], F32, name="ident")
+        planes = [keep.tile([P, T], F32, name=f"plane{j}") for j in range(4)]
+        w1_sb = keep.tile([P, E, 2 * H], U8, name="w1_sb", align_bytes=64)
+        w3_sb = keep.tile([P, E, 2 * H], U8, name="w3_sb", align_bytes=64)
+        w2_sb = keep.tile([P, E, 2 * N], U8, name="w2_sb", align_bytes=64)
+        s1_sb = keep.tile([P, E, H], U8, name="s1_sb", align_bytes=64)
+        s3_sb = keep.tile([P, E, H], U8, name="s3_sb", align_bytes=64)
+        s2_sb = keep.tile([P, E, N], U8, name="s2_sb", align_bytes=64)
+        gate_sb = keep.tile([P, 2, E * C], F32, name="gate_sb")
+        wins = [keep.tile([P, T], F32, name=f"win{h}") for h in range(2)]
+        p01 = keep.tile([P, 2, E * C], F32, name="p01")
+        p23 = [keep.tile([P, 2, GS], F32, name=f"p23_{g}") for g in range(G)]
+        x4 = [keep.tile([P, GS, 4], BF16, name=f"x4_{g}", align_bytes=64) for g in range(G)]
+        xq = [keep.tile([P, GS], U32, name=f"xq_{g}", align_bytes=64) for g in range(G)]
+        xs = [keep.tile([P, GS], U8, name=f"xs_{g}", align_bytes=64) for g in range(G)]
+
+        nc.sync.dma_start(offs_sb[:], offs)
+        xv = xT.rearrange("(p j) t -> p j t", j=4)
+        for j in range(4):
+            nc.sync.dma_start(out=planes[j][:], in_=xv[:, j, :])
+
+        nc.vector.memset(warm[:], 0.0)
+        nc.scalar.activation(warm[:], warm[:], ACT.Sigmoid)
+        for t in (s1_sb, s3_sb, s2_sb):
+            nc.vector.memset(t[:].rearrange("p e i -> p (e i)").bitcast(I32), 0)
+        for w in wins:
+            nc.vector.memset(w[:], 0.0)
+        make_identity(nc, ident[:])
+
+        def load_scales(tile, dram):
+            flat = tile[:].rearrange("p e i -> p (e i)").bitcast(I32)
+            w = tile.shape[2] // 4
+            for q in range(4):
+                nc.sync.dma_start(
+                    out=flat[32 * q : 32 * q + 4, :].rearrange("r (e i) -> r e i", i=w),
+                    in_=dram[:, 0, 4 * q : 4 * q + 4, :].rearrange("e r i -> r e i").bitcast(I32),
+                )
+
+        def load_words(tile, dram, e0, e1):
+            nc.sync.dma_start(
+                out=tile[:, e0:e1, :].bitcast(I32),
+                in_=dram[e0:e1, 0, :, :].rearrange("e p b -> p e b").bitcast(I32),
+            )
+
+        load_scales(s1_sb, w1_scales)
+        load_scales(s3_sb, w3_scales)
+        load_words(w1_sb, w1_words, 0, 2)
+        load_words(w3_sb, w3_words, 0, 2)
+        load_words(w1_sb, w1_words, 2, 4)
+        load_words(w3_sb, w3_words, 2, 4)
+        load_scales(s2_sb, w2_scales)
+        load_words(w2_sb, w2_words, 0, 6)
+        nc.sync.dma_start(dst_sb[:], dst)
+        load_words(w1_sb, w1_words, 4, 6)
+        load_words(w3_sb, w3_words, 4, 6)
+        nc.sync.dma_start(out=gate_sb[:], in_=gate.rearrange("(h p) j -> p h j", p=P))
+
+        for j in range(2):
+            nc.vector.tensor_copy(p01[:, j, :], planes[j][:].indirect(offs_sb[:]))
+        for g in range(G):
+            nc.scalar.copy(x4[g][:, :, 0:2], p01[:, :, GS * g : GS * (g + 1)].rearrange("p t c -> p c t"))
+        for g in range(G):
+            nc.vector.tensor_copy(p23[g][:, 0, :], planes[2][:].indirect(offs_sb[:, GO * g : GO * (g + 1)]))
+
+        def gather3(g):
+            nc.vector.tensor_copy(p23[g][:, 1, :], planes[3][:].indirect(offs_sb[:, GO * g : GO * (g + 1)]))
+
+        def cast(g, eng):
+            o, i = x4[g][:, :, 2:4], p23[g][:].rearrange("p t c -> p c t")
+            if eng == 0:
+                nc.vector.tensor_copy(o, i)
+            else:
+                nc.scalar.copy(o, i)
+
+        def quant(g):
+            nc.vector.quantize_mx(
+                out=xq[g][:].bitcast(FP8X4), scales=xs[g][:], in_=x4[g][:].rearrange("p c t -> p (c t)")
+            )
+
+        gather3(0)
+        gather3(1)
+        cast(0, 0)
+        gather3(2)
+        quant(0)
+        cast(1, 1)
+        quant(1)
+        cast(2, 1)
+        quant(2)
+
+        hs = {}
+
+        def first(e):
+            g, c = divmod(e, 2)
+            cols = slice(C * c, C * (c + 1))
+            res = []
+            for name, w, s in (("a", w1_sb, s1_sb), ("b", w3_sb, s3_sb)):
+                acc = psum.tile([P, H], F32, name=name)
+                nc.tensor.matmul_mx(
+                    out=acc[:],
+                    lhsT=xq[g][:, cols].bitcast(FP8X4),
+                    lhsT_scale=xs[g][:, cols],
+                    rhs=w[:, e, :].bitcast(FP4X4),
+                    rhs_scale=s[:, e, :],
+                    start=True,
+                    stop=True,
+                )
+                res.append(acc)
+            sg = work.tile([P, H], F32, name="sg")
+            nc.scalar.activation(sg[:], res[0][:], ACT.Sigmoid)
+            h = keep.tile([P, H], BF16, name=f"h{e}")
+            nc.vector.tensor_tensor(h[:], res[1][:], sg[:], MULT)
+            hs[e] = h
+
+        def second(g):
+            tp = psum.tile([P, 2, 2, C], F32, name="tp")
+            for c in range(2):
+                words = hs[2 * g + c][:].bitcast(F32)
+                for u in range(2):
+                    nc.tensor.transpose(tp[:, c, u, :], words[:, u::2], ident[:])
+            h4 = work.tile([P, 2, C, 4], BF16, name="h4", align_bytes=64)
+            h4w = h4[:].rearrange("p e c t -> p (e c t)")
+            nc.scalar.copy(
+                h4w.bitcast(F32).rearrange("p (e c u) -> p e c u", e=2, u=2), tp[:].rearrange("p e u c -> p e c u")
+            )
+            hq = work.tile([P, GS], U32, name="hq", align_bytes=64)
+            hsc = work.tile([P, GS], U8, name="hsc", align_bytes=64)
+            nc.vector.quantize_mx(out=hq[:].bitcast(FP8X4), scales=hsc[:], in_=h4w)
+            y = psum.tile([P, 2, GS], F32, name="y")
+            for c in range(2):
+                cols = slice(C * c, C * (c + 1))
+                for n in range(2):
+                    nc.tensor.matmul_mx(
+                        out=y[:, n, cols],
+                        lhsT=w2_sb[:, 2 * g + c, 2 * P * n : 2 * P * (n + 1)].bitcast(FP4X4),
+                        lhsT_scale=s2_sb[:, 2 * g + c, P * n : P * (n + 1)],
+                        rhs=hq[:, cols].bitcast(FP8X4),
+                        rhs_scale=hsc[:, cols],
+                        start=True,
+                        stop=True,
+                    )
+            y_sb = work.tile([P, 2, GS], F32, name="y_sb")
+            nc.scalar.copy(y_sb[:], y[:])
+            return y_sb
+
+        def scatter(g, y_sb):
+            for n in range(2):
+                nc.vector.tensor_tensor(
+                    wins[n][:].indirect(dst_sb[:, GO * g : GO * (g + 1)]),
+                    y_sb[:, n, :],
+                    gate_sb[:, n, GS * g : GS * (g + 1)],
+                    MULT,
+                )
+                if g == G - 1:
+                    nc.sync.dma_start(out[P * n : P * (n + 1), :], wins[n][:])
+
+        first(0)
+        first(1)
+        first(2)
+        first(3)
+        y0 = second(0)
+        first(4)
+        first(5)
+        scatter(0, y0)
+        y1 = second(1)
+        scatter(1, y1)
+        y2 = second(2)
+        scatter(2, y2)

@@ -79,18 +79,18 @@ def tile_moe_two_glu_sigmoid_kernel(
                 in_=dram[e0:e1, 0, :, :].rearrange("e p b -> p e b").bitcast(I32),
             )
 
-        load_scales(s1_sb, w1_scales)
-        load_scales(s3_sb, w3_scales)
         load_words(w1_sb, w1_words, 0, 2)
         load_words(w3_sb, w3_words, 0, 2)
+        load_scales(s1_sb, w1_scales)
+        load_scales(s3_sb, w3_scales)
         load_words(w1_sb, w1_words, 2, 4)
         load_words(w3_sb, w3_words, 2, 4)
         load_scales(s2_sb, w2_scales)
         load_words(w2_sb, w2_words, 0, 6)
         nc.sync.dma_start(dst_sb[:], dst)
+        nc.sync.dma_start(out=gate_sb[:], in_=gate.rearrange("(h p) j -> p h j", p=P))
         load_words(w1_sb, w1_words, 4, 6)
         load_words(w3_sb, w3_words, 4, 6)
-        nc.sync.dma_start(out=gate_sb[:], in_=gate.rearrange("(h p) j -> p h j", p=P))
 
         for j in range(2):
             nc.vector.tensor_copy(p01[:, j, :], planes[j][:].indirect(offs_sb[:]))
@@ -176,17 +176,12 @@ def tile_moe_two_glu_sigmoid_kernel(
                         stop=True,
                     )
             y_sb = work.tile([P, 2, GS], F32, name="y_sb")
-            nc.scalar.copy(y_sb[:], y[:])
+            nc.vector.tensor_tensor(y_sb[:], y[:], gate_sb[:, :, GS * g : GS * (g + 1)], MULT)
             return y_sb
 
         def scatter(g, y_sb):
             for n in range(2):
-                nc.vector.tensor_tensor(
-                    wins[n][:].indirect(dst_sb[:, GO * g : GO * (g + 1)]),
-                    y_sb[:, n, :],
-                    gate_sb[:, n, GS * g : GS * (g + 1)],
-                    MULT,
-                )
+                nc.vector.tensor_copy(wins[n][:].indirect(dst_sb[:, GO * g : GO * (g + 1)]), y_sb[:, n, :])
                 if g == G - 1:
                     nc.sync.dma_start(out[P * n : P * (n + 1), :], wins[n][:])
 

@@ -61,7 +61,7 @@ def tile_moe_two_glu_sigmoid_kernel(
         for t in (s1_sb, s3_sb, s2_sb):
             nc.vector.memset(t[:].rearrange("p e i -> p (e i)").bitcast(I32), 0)
         for w in wins:
-            nc.vector.memset(w[:], 0.0)
+            nc.gpsimd.memset(w[:], 0.0)
         make_identity(nc, ident[:])
 
         def load_scales(tile, dram):
@@ -80,88 +80,90 @@ def tile_moe_two_glu_sigmoid_kernel(
             )
 
         load_words(w1_sb, w1_words, 0, 2)
-        load_words(w3_sb, w3_words, 0, 2)
         load_scales(s1_sb, w1_scales)
+        load_words(w3_sb, w3_words, 0, 2)
         load_scales(s3_sb, w3_scales)
         load_words(w1_sb, w1_words, 2, 4)
         load_words(w3_sb, w3_words, 2, 4)
+        load_words(w1_sb, w1_words, 4, 6)
+        load_words(w3_sb, w3_words, 4, 6)
         load_scales(s2_sb, w2_scales)
         load_words(w2_sb, w2_words, 0, 6)
         nc.sync.dma_start(dst_sb[:], dst)
         nc.sync.dma_start(out=gate_sb[:], in_=gate.rearrange("(h p) j -> p h j", p=P))
-        load_words(w1_sb, w1_words, 4, 6)
-        load_words(w3_sb, w3_words, 4, 6)
 
-        for j in range(2):
-            nc.vector.tensor_copy(p01[:, j, :], planes[j][:].indirect(offs_sb[:]))
-        for g in range(G):
+        def gather(j, g):
+            nc.vector.tensor_copy(p23[g][:, j - 2, :], planes[j][:].indirect(offs_sb[:, GO * g : GO * (g + 1)]))
+
+        def precast(g):
             nc.scalar.copy(x4[g][:, :, 0:2], p01[:, :, GS * g : GS * (g + 1)].rearrange("p t c -> p c t"))
-        for g in range(G):
-            nc.vector.tensor_copy(p23[g][:, 0, :], planes[2][:].indirect(offs_sb[:, GO * g : GO * (g + 1)]))
-
-        def gather3(g):
-            nc.vector.tensor_copy(p23[g][:, 1, :], planes[3][:].indirect(offs_sb[:, GO * g : GO * (g + 1)]))
 
         def cast(g, eng):
-            o, i = x4[g][:, :, 2:4], p23[g][:].rearrange("p t c -> p c t")
-            if eng == 0:
-                nc.vector.tensor_copy(o, i)
+            dst_ap, src_ap = x4[g][:, :, 2:4], p23[g][:].rearrange("p t c -> p c t")
+            if eng == "V":
+                nc.vector.tensor_copy(dst_ap, src_ap)
+            elif eng == "G":
+                nc.gpsimd.tensor_scalar(dst_ap, src_ap, 1.0, 0.0, MULT, mybir.AluOpType.add)
             else:
-                nc.scalar.copy(o, i)
+                nc.scalar.copy(dst_ap, src_ap)
 
         def quant(g):
             nc.vector.quantize_mx(
                 out=xq[g][:].bitcast(FP8X4), scales=xs[g][:], in_=x4[g][:].rearrange("p c t -> p (c t)")
             )
 
-        gather3(0)
-        gather3(1)
-        cast(0, 0)
-        gather3(2)
-        quant(0)
-        cast(1, 1)
-        quant(1)
-        cast(2, 1)
-        quant(2)
+        acc, sig, hid, turned, h4s, hqs, ys, ysb = {}, {}, {}, {}, {}, {}, {}, {}
 
-        hs = {}
-
-        def first(e):
+        def first(e, name, w, s):
             g, c = divmod(e, 2)
             cols = slice(C * c, C * (c + 1))
-            res = []
-            for name, w, s in (("a", w1_sb, s1_sb), ("b", w3_sb, s3_sb)):
-                acc = psum.tile([P, H], F32, name=name)
-                nc.tensor.matmul_mx(
-                    out=acc[:],
-                    lhsT=xq[g][:, cols].bitcast(FP8X4),
-                    lhsT_scale=xs[g][:, cols],
-                    rhs=w[:, e, :].bitcast(FP4X4),
-                    rhs_scale=s[:, e, :],
-                    start=True,
-                    stop=True,
-                )
-                res.append(acc)
-            sg = work.tile([P, H], F32, name="sg")
-            nc.scalar.activation(sg[:], res[0][:], ACT.Sigmoid)
-            h = keep.tile([P, H], BF16, name=f"h{e}")
-            nc.vector.tensor_tensor(h[:], res[1][:], sg[:], MULT)
-            hs[e] = h
+            t = psum.tile([P, H], F32, name=name)
+            nc.tensor.matmul_mx(
+                out=t[:],
+                lhsT=xq[g][:, cols].bitcast(FP8X4),
+                lhsT_scale=xs[g][:, cols],
+                rhs=w[:, e, :].bitcast(FP4X4),
+                rhs_scale=s[:, e, :],
+                start=True,
+                stop=True,
+            )
+            acc[name, e] = t
 
-        def second(g):
+        def sigm(e):
+            sg = work.tile([P, H], F32, name="sg")
+            nc.scalar.activation(sg[:], acc["a", e][:], ACT.Sigmoid)
+            sig[e] = sg
+
+        def mul(e):
+            h = keep.tile([P, H], BF16, name=f"h{e}")
+            nc.vector.tensor_tensor(h[:], acc["b", e][:], sig[e][:], MULT)
+            hid[e] = h
+
+        def turn(g):
             tp = psum.tile([P, 2, 2, C], F32, name="tp")
             for c in range(2):
-                words = hs[2 * g + c][:].bitcast(F32)
+                words = hid[2 * g + c][:].bitcast(F32)
                 for u in range(2):
                     nc.tensor.transpose(tp[:, c, u, :], words[:, u::2], ident[:])
+            turned[g] = tp
+
+        def evt(g):
             h4 = work.tile([P, 2, C, 4], BF16, name="h4", align_bytes=64)
             h4w = h4[:].rearrange("p e c t -> p (e c t)")
             nc.scalar.copy(
-                h4w.bitcast(F32).rearrange("p (e c u) -> p e c u", e=2, u=2), tp[:].rearrange("p e u c -> p e c u")
+                h4w.bitcast(F32).rearrange("p (e c u) -> p e c u", e=2, u=2),
+                turned[g][:].rearrange("p e u c -> p e c u"),
             )
+            h4s[g] = h4w
+
+        def hquant(g):
             hq = work.tile([P, GS], U32, name="hq", align_bytes=64)
             hsc = work.tile([P, GS], U8, name="hsc", align_bytes=64)
-            nc.vector.quantize_mx(out=hq[:].bitcast(FP8X4), scales=hsc[:], in_=h4w)
+            nc.vector.quantize_mx(out=hq[:].bitcast(FP8X4), scales=hsc[:], in_=h4s[g])
+            hqs[g] = (hq, hsc)
+
+        def second(g):
+            hq, hsc = hqs[g]
             y = psum.tile([P, 2, GS], F32, name="y")
             for c in range(2):
                 cols = slice(C * c, C * (c + 1))
@@ -175,25 +177,82 @@ def tile_moe_two_glu_sigmoid_kernel(
                         start=True,
                         stop=True,
                     )
+            ys[g] = y
+
+        def evy(g):
             y_sb = work.tile([P, 2, GS], F32, name="y_sb")
-            nc.vector.tensor_tensor(y_sb[:], y[:], gate_sb[:, :, GS * g : GS * (g + 1)], MULT)
-            return y_sb
+            nc.scalar.copy(y_sb[:], ys[g][:])
+            ysb[g] = y_sb
 
-        def scatter(g, y_sb):
-            for n in range(2):
-                nc.vector.tensor_copy(wins[n][:].indirect(dst_sb[:, GO * g : GO * (g + 1)]), y_sb[:, n, :])
-                if g == G - 1:
-                    nc.sync.dma_start(out[P * n : P * (n + 1), :], wins[n][:])
+        def scatter(g, n):
+            nc.vector.tensor_tensor(
+                wins[n][:].indirect(dst_sb[:, GO * g : GO * (g + 1)]),
+                ysb[g][:, n, :],
+                gate_sb[:, n, GS * g : GS * (g + 1)],
+                MULT,
+            )
+            if g == G - 1:
+                nc.sync.dma_start(out[P * n : P * (n + 1), :], wins[n][:])
 
-        first(0)
-        first(1)
-        first(2)
-        first(3)
-        y0 = second(0)
-        first(4)
-        first(5)
-        scatter(0, y0)
-        y1 = second(1)
-        scatter(1, y1)
-        y2 = second(2)
-        scatter(2, y2)
+        nc.vector.tensor_copy(p01[:, 0, :], planes[0][:].indirect(offs_sb[:]))
+        nc.vector.tensor_copy(p01[:, 1, :], planes[1][:].indirect(offs_sb[:]))
+        precast(0)
+        precast(1)
+        precast(2)
+        gather(2, 0)
+        gather(2, 1)
+        gather(3, 0)
+        cast(0, "S")
+        gather(3, 1)
+        cast(1, "S")
+        gather(3, 2)
+        quant(0)
+        gather(2, 2)
+        quant(1)
+        first(0, "a", w1_sb, s1_sb)
+        first(1, "a", w1_sb, s1_sb)
+        first(0, "b", w3_sb, s3_sb)
+        first(1, "b", w3_sb, s3_sb)
+        sigm(0)
+        sigm(1)
+        mul(0)
+        mul(1)
+        first(2, "a", w1_sb, s1_sb)
+        sigm(2)
+        cast(2, "S")
+        quant(2)
+        first(3, "a", w1_sb, s1_sb)
+        first(2, "b", w3_sb, s3_sb)
+        first(3, "b", w3_sb, s3_sb)
+        sigm(3)
+        mul(2)
+        mul(3)
+        turn(0)
+        evt(0)
+        hquant(0)
+        first(4, "a", w1_sb, s1_sb)
+        first(5, "a", w1_sb, s1_sb)
+        first(4, "b", w3_sb, s3_sb)
+        first(5, "b", w3_sb, s3_sb)
+        sigm(4)
+        sigm(5)
+        mul(4)
+        mul(5)
+        second(0)
+        evy(0)
+        turn(1)
+        evt(1)
+        turn(2)
+        evt(2)
+        scatter(0, 0)
+        hquant(1)
+        hquant(2)
+        second(1)
+        second(2)
+        evy(1)
+        evy(2)
+        scatter(0, 1)
+        scatter(1, 0)
+        scatter(2, 0)
+        scatter(1, 1)
+        scatter(2, 1)

from contextlib import ExitStack

import concourse.mybir as mybir
from concourse.masks import make_identity

K, T, E, C, H, N = 512, 1536, 6, 128, 512, 256
FLOPS = 2 * E * C * (2 * K * H + H * N)

F32 = mybir.dt.float32
BF16 = mybir.dt.bfloat16
I32 = mybir.dt.int32
U32 = mybir.dt.uint32
U16 = mybir.dt.uint16
U8 = mybir.dt.uint8
FP8X4 = mybir.dt.float8_e4m3fn_x4
FP4X4 = mybir.dt.float4_e2m1fn_x4
ACT = mybir.ActivationFunctionType
MULT = mybir.AluOpType.mult

P = 128
G = 3
GS = 2 * C
GO = GS // 16


def tile_moe_two_glu_sigmoid_kernel(
    tc, xT, w1_words, w1_scales, w3_words, w3_scales, w2_words, w2_scales, gate, offs, dst, out
):
    nc = tc.nc
    with ExitStack() as ctx:
        keep = ctx.enter_context(tc.tile_pool(name="keep", bufs=1))
        work = ctx.enter_context(tc.tile_pool(name="work", bufs=3))
        psum = ctx.enter_context(tc.psum_pool(name="psum", bufs=2))

        offs_sb = keep.tile([P, E * C // 16], U16, name="offs_sb")
        dst_sb = keep.tile([P, E * C // 16], U16, name="dst_sb")
        warm = keep.tile([P, 1], F32, name="warm")
        ident = keep.tile([P, P], F32, name="ident")
        planes = [keep.tile([P, T], F32, name=f"plane{j}") for j in range(4)]
        w1_sb = keep.tile([P, E, 2 * H], U8, name="w1_sb", align_bytes=64)
        w3_sb = keep.tile([P, E, 2 * H], U8, name="w3_sb", align_bytes=64)
        w2_sb = keep.tile([P, E, 2 * N], U8, name="w2_sb", align_bytes=64)
        s1_sb = keep.tile([P, E, H], U8, name="s1_sb", align_bytes=64)
        s3_sb = keep.tile([P, E, H], U8, name="s3_sb", align_bytes=64)
        s2_sb = keep.tile([P, E, N], U8, name="s2_sb", align_bytes=64)
        gate_sb = keep.tile([P, 2, E * C], F32, name="gate_sb")
        wins = [keep.tile([P, T], F32, name=f"win{h}") for h in range(2)]
        p01 = keep.tile([P, 2, E * C], F32, name="p01")
        p23 = [keep.tile([P, 2, GS], F32, name=f"p23_{g}") for g in range(G)]
        x4 = [keep.tile([P, GS, 4], BF16, name=f"x4_{g}", align_bytes=64) for g in range(G)]
        xq = [keep.tile([P, GS], U32, name=f"xq_{g}", align_bytes=64) for g in range(G)]
        xs = [keep.tile([P, GS], U8, name=f"xs_{g}", align_bytes=64) for g in range(G)]

        nc.sync.dma_start(offs_sb[:], offs)
        xv = xT.rearrange("(p j) t -> p j t", j=4)
        for j in range(4):
            nc.sync.dma_start(out=planes[j][:], in_=xv[:, j, :])

        nc.vector.memset(warm[:], 0.0)
        nc.scalar.activation(warm[:], warm[:], ACT.Sigmoid)
        for t in (s1_sb, s3_sb, s2_sb):
            nc.vector.memset(t[:].rearrange("p e i -> p (e i)").bitcast(I32), 0)
        for w in wins:
            nc.gpsimd.memset(w[:], 0.0)
        make_identity(nc, ident[:])

        def load_scales(tile, dram):
            flat = tile[:].rearrange("p e i -> p (e i)").bitcast(I32)
            w = tile.shape[2] // 4
            for q in range(4):
                nc.sync.dma_start(
                    out=flat[32 * q : 32 * q + 4, :].rearrange("r (e i) -> r e i", i=w),
                    in_=dram[:, 0, 4 * q : 4 * q + 4, :].rearrange("e r i -> r e i").bitcast(I32),
                )

        def load_words(tile, dram, e0, e1):
            nc.sync.dma_start(
                out=tile[:, e0:e1, :].bitcast(I32),
                in_=dram[e0:e1, 0, :, :].rearrange("e p b -> p e b").bitcast(I32),
            )

        load_words(w1_sb, w1_words, 0, 2)
        load_scales(s1_sb, w1_scales)
        load_words(w3_sb, w3_words, 0, 2)
        load_scales(s3_sb, w3_scales)
        load_words(w1_sb, w1_words, 2, 4)
        load_words(w3_sb, w3_words, 2, 4)
        load_words(w1_sb, w1_words, 4, 6)
        load_words(w3_sb, w3_words, 4, 6)
        load_scales(s2_sb, w2_scales)
        load_words(w2_sb, w2_words, 0, 6)
        nc.sync.dma_start(dst_sb[:], dst)
        nc.sync.dma_start(out=gate_sb[:], in_=gate.rearrange("(h p) j -> p h j", p=P))

        def gather(j, g):
            nc.vector.tensor_copy(p23[g][:, j - 2, :], planes[j][:].indirect(offs_sb[:, GO * g : GO * (g + 1)]))

        def precast(g):
            nc.scalar.copy(x4[g][:, :, 0:2], p01[:, :, GS * g : GS * (g + 1)].rearrange("p t c -> p c t"))

        def cast(g, eng):
            dst_ap, src_ap = x4[g][:, :, 2:4], p23[g][:].rearrange("p t c -> p c t")
            if eng == "V":
                nc.vector.tensor_copy(dst_ap, src_ap)
            elif eng == "G":
                nc.gpsimd.tensor_scalar(dst_ap, src_ap, 1.0, 0.0, MULT, mybir.AluOpType.add)
            else:
                nc.scalar.copy(dst_ap, src_ap)

        def quant(g):
            nc.vector.quantize_mx(
                out=xq[g][:].bitcast(FP8X4), scales=xs[g][:], in_=x4[g][:].rearrange("p c t -> p (c t)")
            )

        acc, sig, hid, turned, h4s, hqs, ys, ysb = {}, {}, {}, {}, {}, {}, {}, {}

        def first(e, name, w, s):
            g, c = divmod(e, 2)
            cols = slice(C * c, C * (c + 1))
            t = psum.tile([P, H], F32, name=name)
            nc.tensor.matmul_mx(
                out=t[:],
                lhsT=xq[g][:, cols].bitcast(FP8X4),
                lhsT_scale=xs[g][:, cols],
                rhs=w[:, e, :].bitcast(FP4X4),
                rhs_scale=s[:, e, :],
                start=True,
                stop=True,
            )
            acc[name, e] = t

        def sigm(e):
            sg = work.tile([P, H], F32, name="sg")
            nc.scalar.activation(sg[:], acc["a", e][:], ACT.Sigmoid)
            sig[e] = sg

        def mul(e):
            h = keep.tile([P, H], BF16, name=f"h{e}")
            nc.vector.tensor_tensor(h[:], acc["b", e][:], sig[e][:], MULT)
            hid[e] = h

        def turn(g):
            tp = psum.tile([P, 2, 2, C], F32, name="tp")
            for c in range(2):
                words = hid[2 * g + c][:].bitcast(F32)
                for u in range(2):
                    nc.tensor.transpose(tp[:, c, u, :], words[:, u::2], ident[:])
            turned[g] = tp

        def evt(g):
            h4 = work.tile([P, 2, C, 4], BF16, name="h4", align_bytes=64)
            h4w = h4[:].rearrange("p e c t -> p (e c t)")
            nc.scalar.copy(
                h4w.bitcast(F32).rearrange("p (e c u) -> p e c u", e=2, u=2),
                turned[g][:].rearrange("p e u c -> p e c u"),
            )
            h4s[g] = h4w

        def hquant(g):
            hq = work.tile([P, GS], U32, name="hq", align_bytes=64)
            hsc = work.tile([P, GS], U8, name="hsc", align_bytes=64)
            nc.vector.quantize_mx(out=hq[:].bitcast(FP8X4), scales=hsc[:], in_=h4s[g])
            hqs[g] = (hq, hsc)

        def second(g):
            hq, hsc = hqs[g]
            y = psum.tile([P, 2, GS], F32, name="y")
            for c in range(2):
                cols = slice(C * c, C * (c + 1))
                for n in range(2):
                    nc.tensor.matmul_mx(
                        out=y[:, n, cols],
                        lhsT=w2_sb[:, 2 * g + c, 2 * P * n : 2 * P * (n + 1)].bitcast(FP4X4),
                        lhsT_scale=s2_sb[:, 2 * g + c, P * n : P * (n + 1)],
                        rhs=hq[:, cols].bitcast(FP8X4),
                        rhs_scale=hsc[:, cols],
                        start=True,
                        stop=True,
                    )
            ys[g] = y

        def evy(g):
            y_sb = work.tile([P, 2, GS], F32, name="y_sb")
            nc.scalar.copy(y_sb[:], ys[g][:])
            ysb[g] = y_sb

        def scatter(g, n):
            nc.vector.tensor_tensor(
                wins[n][:].indirect(dst_sb[:, GO * g : GO * (g + 1)]),
                ysb[g][:, n, :],
                gate_sb[:, n, GS * g : GS * (g + 1)],
                MULT,
            )
            if g == G - 1:
                nc.sync.dma_start(out[P * n : P * (n + 1), :], wins[n][:])

        nc.vector.tensor_copy(p01[:, 0, :], planes[0][:].indirect(offs_sb[:]))
        nc.vector.tensor_copy(p01[:, 1, :], planes[1][:].indirect(offs_sb[:]))
        precast(0)
        precast(1)
        precast(2)
        gather(2, 0)
        gather(2, 1)
        gather(3, 0)
        cast(0, "S")
        gather(3, 1)
        cast(1, "S")
        gather(3, 2)
        quant(0)
        gather(2, 2)
        quant(1)
        first(0, "a", w1_sb, s1_sb)
        first(1, "a", w1_sb, s1_sb)
        first(0, "b", w3_sb, s3_sb)
        first(1, "b", w3_sb, s3_sb)
        sigm(0)
        sigm(1)
        mul(0)
        mul(1)
        first(2, "a", w1_sb, s1_sb)
        sigm(2)
        cast(2, "S")
        quant(2)
        first(3, "a", w1_sb, s1_sb)
        first(2, "b", w3_sb, s3_sb)
        first(3, "b", w3_sb, s3_sb)
        sigm(3)
        mul(2)
        mul(3)
        turn(0)
        evt(0)
        hquant(0)
        first(4, "a", w1_sb, s1_sb)
        first(5, "a", w1_sb, s1_sb)
        first(4, "b", w3_sb, s3_sb)
        first(5, "b", w3_sb, s3_sb)
        sigm(4)
        sigm(5)
        mul(4)
        mul(5)
        second(0)
        evy(0)
        turn(1)
        evt(1)
        turn(2)
        evt(2)
        scatter(0, 0)
        hquant(1)
        hquant(2)
        second(1)
        second(2)
        evy(1)
        evy(2)
        scatter(0, 1)
        scatter(1, 0)
        scatter(2, 0)
        scatter(1, 1)
        scatter(2, 1)
